import numpy as np
import ml_dtypes


def mxq(x, axis, fmt="e4m3"):
    dtype, down = {"e4m3": (ml_dtypes.float8_e4m3fn, 7), "e5m2": (ml_dtypes.float8_e5m2, 14)}[fmt]
    v = np.moveaxis(np.asarray(x, np.float32).astype(ml_dtypes.bfloat16).astype(np.float64), axis, -1)
    blocks = v.reshape(v.shape[:-1] + (-1, 32))
    amax = np.abs(blocks).max(-1, keepdims=True)
    byte = np.maximum(np.where(amax > 0, np.frexp(amax)[1] - 1 + 127, 0) - down, 1)
    scale = np.exp2(byte - 127.0)
    codes = (blocks / scale).astype(np.float32).astype(dtype).astype(np.float64)
    return np.moveaxis((codes * scale).reshape(v.shape), -1, axis)


WIDE = False


def mx_kscale(k):
    if not WIDE:
        return np.ones(k)
    levels = np.array([10, -10, 5, -5, 0])
    if k % 512:
        return np.exp2(np.random.permutation(np.resize(levels, k // 32))).repeat(32)
    a = np.empty((k // 512, 16))
    for p in range(k // 512):
        a[p, :8] = np.random.permutation(np.resize(levels, 8))
        for g in range(8):
            far = levels[np.abs(levels - a[p, g]) >= 10]
            a[p, g + 8] = far[np.random.randint(len(far))]
    return np.exp2(a.ravel()).repeat(32)


def f64(x):
    return np.asarray(x).astype(np.float64)


def striped(idx):
    return np.tile(idx.reshape(-1, 16).T, (8, 1)).astype(np.uint16)


def unstriped(offs):
    return offs[:16].T.reshape(-1).astype(np.int64)


def striped8(idx):
    return np.concatenate([x.reshape(-1, 16).T for x in idx]).astype(np.uint16)


def runs(offs, k):
    lists = np.stack([offs[16 * r : 16 * r + 16].T.reshape(-1) for r in range(8)]).astype(np.int64)
    return lists[np.arange(k) % 512 // 64]


def pack_weight(w):
    k, n = w.shape
    w = f64(np.asarray(w, np.float32).astype(ml_dtypes.bfloat16)).reshape(k // 32, 32, n)
    amax = np.abs(w).max(1)
    byte = np.clip(np.where(amax > 0, np.frexp(amax)[1] - 1 + 127 - 7, 1), 1, 254)
    scaled = (w * np.exp2(127.0 - byte)[:, None, :]).reshape(k, n).astype(np.float32)
    words = np.ascontiguousarray(scaled.reshape(k // 512, 128, 4, n).transpose(0, 1, 3, 2)).astype(ml_dtypes.float8_e4m3fn).view(np.uint8)
    return words, np.ascontiguousarray(byte.astype(np.uint8).reshape(k // 512, 16, n))


def unpack_weight(words, scales):
    g, p, n, _ = words.shape
    vals = np.ascontiguousarray(words).view(ml_dtypes.float8_e4m3fn).astype(np.float64) * np.repeat(np.exp2(scales.astype(np.float64) - 127.0), 8, axis=1)[..., None]
    return vals.transpose(0, 1, 3, 2).reshape(g * 512, n)


K, T, S, H, G = 512, 2048, 512, 512, 2048


def setup_inputs():
    n = np.random.standard_normal
    s = mx_kscale(K)[:, None]
    packed_xT = pack_weight(n((K, T)) * s)
    packed_dT = pack_weight(n((K, G)) / s)
    return {
        "x_words": packed_xT[0],
        "x_scales": packed_xT[1],
        "w1": (n((K, H)) / np.sqrt(K) / s).astype(np.float32),
        "gs": (np.random.uniform(0.5, 1.5, (K, 1)) * s).astype(np.float32),
        "d_words": packed_dT[0],
        "d_scales": packed_dT[1],
        "offs": striped(np.random.permutation(T)[:S]),
        "n1": striped8(np.stack([np.random.permutation(S) for _ in range(8)])),
        "n2": striped8(np.stack([np.random.permutation(S) for _ in range(8)])),
        "k1": striped8(np.random.randint(0, G, (8, H))),
        "n3": striped8(np.stack([np.random.permutation(S) for _ in range(8)])),
        "n4": striped8(np.stack([np.random.permutation(S) for _ in range(8)])),
    }


def reference(x_words, x_scales, w1, gs, d_words, d_scales, offs, n1, n2, k1, n3, n4):
    d_k1 = unpack_weight(d_words, d_scales)[np.arange(K)[:, None], runs(k1, K)]
    xq = unpack_weight(x_words, x_scales)[:, unstriped(offs)]
    y = mxq(f64(w1), 0, "e4m3").T @ xq
    z = f64(gs) * (y[np.arange(H)[:, None], runs(n1, H)] + 0.75 * (y[np.arange(H)[:, None], runs(n2, H)]))
    h = 0.0625 * ((d_k1.T @ mxq(z, 0, "e4m3")))
    st = h - (h[np.arange(H)[:, None], runs(n3, H)])
    return np.maximum(st, st[np.arange(H)[:, None], runs(n4, H)])

@@ -1,0 +1,220 @@
+from contextlib import ExitStack
+
+import concourse.mybir as mybir
+
+K, T, S, H, G = 512, 2048, 512, 512, 2048
+FLOPS = 2 * K * H * S + 2 * K * H * S
+
+F32 = mybir.dt.float32
+BF16 = mybir.dt.bfloat16
+I32 = mybir.dt.int32
+U32 = mybir.dt.uint32
+U16 = mybir.dt.uint16
+U8 = mybir.dt.uint8
+FP8X4 = mybir.dt.float8_e4m3fn_x4
+COPY = mybir.ActivationFunctionType.Copy
+MULT = mybir.AluOpType.mult
+ADD = mybir.AluOpType.add
+MAX = mybir.AluOpType.max
+
+P = 128
+PACK = 4
+HALF = S // 2
+LCOL = HALF // 16
+
+
+def tile_picked_densesumhopmx_none_p_kernel(
+    tc, x_words, x_scales, w1, gs, d_words, d_scales, offs, n1, n2, k1, n3, n4, out
+):
+    nc = tc.nc
+    with ExitStack() as ctx:
+        lists = ctx.enter_context(tc.tile_pool(name="lists", bufs=1))
+        sb = ctx.enter_context(tc.tile_pool(name="sb", bufs=1))
+        psum = ctx.enter_context(tc.psum_pool(name="psum", bufs=1))
+
+        def cols(h):
+            return slice(h * HALF, (h + 1) * HALF)
+
+        def entries(tile, h):
+            return tile[:, h * LCOL : (h + 1) * LCOL]
+
+        def load_list(name, src):
+            tile = lists.tile([P, S // 16], U16, name=name)
+            nc.sync.dma_start(tile[:], src)
+            return tile
+
+        xs_win = sb.tile([P, T], U8, align_bytes=64)
+        nc.gpsimd.memset(xs_win[:].bitcast(I32), 0)
+        ds_win = sb.tile([P, G], U8, align_bytes=64)
+        nc.vector.memset(ds_win[:].bitcast(I32), 0)
+        d_planes = sb.tile([P, H], U8, align_bytes=64)
+        nc.gpsimd.memset(d_planes[:].bitcast(I32), 0)
+
+        w_rows = w1.rearrange("(p j) c -> p j c", j=PACK)
+        w_raw = [sb.tile([P, PACK, HALF], F32, name=f"w_raw{h}", align_bytes=64) for h in range(2)]
+        nc.sync.dma_start(w_raw[0][:], w_rows[:, :, cols(0)])
+        offs_t = load_list("offs_t", offs)
+        xs_rows = x_scales[0].rearrange("(q i) c -> i q c", i=4)
+        for i in range(4):
+            nc.sync.dma_start(xs_win[i:P:32, :].bitcast(I32), xs_rows[i].bitcast(I32))
+        nc.sync.dma_start(w_raw[1][:], w_rows[:, :, cols(1)])
+        xw_win = sb.tile([P, T], U32, align_bytes=64)
+        nc.sync.dma_start(xw_win[:].bitcast(I32), x_words[0].rearrange("p c r -> p (c r)").bitcast(I32))
+        k1_t = load_list("k1_t", k1)
+        ds_rows = d_scales[0].rearrange("(g e) c -> e g c", e=2)
+        for e in range(2):
+            nc.sync.dma_start(ds_win[e:P:16, :].bitcast(I32), ds_rows[e].bitcast(I32))
+        gs_t = sb.tile([P, PACK], F32, align_bytes=64)
+        nc.sync.dma_start(gs_t[:], gs.rearrange("(p t) o -> p (t o)", t=PACK))
+        n2_t = load_list("n2_t", n2)
+        n1_t = load_list("n1_t", n1)
+        dw_win = sb.tile([P, G], U32, align_bytes=64)
+        nc.sync.dma_start(dw_win[:].bitcast(I32), d_words[0].rearrange("p c r -> p (c r)").bitcast(I32))
+        n3_t = load_list("n3_t", n3)
+        n4_t = load_list("n4_t", n4)
+
+        w_bf = sb.tile([P, PACK, P, PACK], BF16, align_bytes=64)
+        for h in range(2):
+            nc.scalar.activation(
+                w_bf[:, :, h * (P // 2) : (h + 1) * (P // 2), :].rearrange("p t m j -> p m j t"),
+                w_raw[h][:].rearrange("p j (m t) -> p m j t", t=PACK),
+                COPY,
+            )
+        xs_pick = sb.tile([P, S], U8, align_bytes=64)
+        nc.vector.tensor_copy(xs_pick[:], xs_win[:].indirect(offs_t[:]))
+        w_codes = sb.tile([P, H], U32, align_bytes=64)
+        w_planes = sb.tile([P, H], U8, align_bytes=64)
+        nc.vector.quantize_mx(
+            out=w_codes[:].bitcast(FP8X4), scales=w_planes[:], in_=w_bf[:].rearrange("p t m j -> p (t m j)")
+        )
+        xw_pick = sb.tile([P, S], U32, align_bytes=64)
+        for h in range(2):
+            nc.vector.tensor_copy(xw_pick[:, cols(h)], xw_win[:].indirect(entries(offs_t, h)))
+
+        ds_pick = sb.tile([P, H], U8, align_bytes=64)
+        nc.vector.tensor_copy(ds_pick[:], ds_win[:].indirect(k1_t[:]))
+        ds_dealt = sb.tile([P, H], U8, align_bytes=64)
+        nc.vector.tensor_copy(
+            ds_dealt[:].rearrange("p (t m) -> p m t", t=PACK), ds_pick[:].rearrange("p (m t) -> p m t", t=PACK)
+        )
+        for odd in range(2):
+            for e in range(2):
+                nc.sync.dma_start(
+                    d_planes[2 * odd + e : P : 32, :].bitcast(I32), ds_dealt[16 * odd + e : P : 32, :].bitcast(I32)
+                )
+
+        y = []
+        for t in range(PACK):
+            y_t = sb.tile([P, S], F32, name=f"y{t}", align_bytes=64)
+            for h in range(2):
+                acc = psum.tile([P, HALF], F32, name=f"acc_y{t}{h}", tag=f"bank{t}{h}")
+                nc.tensor.matmul_mx(
+                    out=acc[:],
+                    lhsT=w_codes[:, t * P : (t + 1) * P].bitcast(FP8X4),
+                    lhsT_scale=w_planes[:, t * P : (t + 1) * P],
+                    rhs=xw_pick[:, cols(h)].bitcast(FP8X4),
+                    rhs_scale=xs_pick[:, cols(h)],
+                    start=True,
+                    stop=True,
+                )
+                nc.scalar.activation(y_t[:, cols(h)], acc[:], COPY, scale=gs_t[:, t : t + 1])
+            y.append(y_t)
+
+        z_codes = sb.tile([P, S], U32, align_bytes=64)
+        z_planes = sb.tile([P, S], U8, align_bytes=64)
+        z = [sb.tile([P, PACK, HALF], F32, name=f"z{h}", align_bytes=64) for h in range(2)]
+        z_bf = [sb.tile([P, HALF, PACK], BF16, name=f"z_bf{h}", align_bytes=64) for h in range(2)]
+        second = {}
+
+        def fetch_second(h, t):
+            tile = sb.tile([P, HALF], F32, name=f"second{h}{t}", tag=f"second{h}{t}", align_bytes=64)
+            nc.vector.tensor_scalar(tile[:], y[t][:].indirect(entries(n2_t, h)), 0.75, 0.0, MULT, ADD)
+            second[(h, t)] = tile
+
+        def fetch_first(h, t):
+            nc.vector.tensor_tensor(z[h][:, t, :], y[t][:].indirect(entries(n1_t, h)), second[(h, t)][:], ADD)
+            if t == PACK - 1:
+                nc.scalar.copy(
+                    z_bf[h][:].rearrange("p (c i) t -> p c t i", i=4),
+                    z[h][:].rearrange("p t (c i) -> p c t i", i=4),
+                )
+
+        def quantise_z(h):
+            nc.vector.quantize_mx(
+                out=z_codes[:, cols(h)].bitcast(FP8X4),
+                scales=z_planes[:, cols(h)],
+                in_=z_bf[h][:].rearrange("p n t -> p (n t)"),
+            )
+
+        steps = [(h, t) for h in range(2) for t in range(PACK)]
+        fetch_second(*steps[0])
+        for s in range(1, len(steps)):
+            fetch_second(*steps[s])
+            fetch_first(*steps[s - 1])
+        fetch_first(*steps[-1])
+        quantise_z(0)
+
+        dw_pick = sb.tile([P, H], U32, tag="second12", align_bytes=64)
+        nc.vector.tensor_copy(dw_pick[:], dw_win[:].indirect(k1_t[:]))
+        d_codes = sb.tile([P, H], U32, align_bytes=64)
+        nc.vector.tensor_copy(
+            d_codes[:].rearrange("p (t m) -> p m t", t=PACK), dw_pick[:].rearrange("p (m t) -> p m t", t=PACK)
+        )
+        quantise_z(1)
+
+        h_neg, h_pos = [], []
+        for t in range(PACK):
+            neg = sb.tile([P, S], F32, name=f"h_neg{t}", align_bytes=64)
+            pos = sb.tile([P, S], F32, name=f"h_pos{t}", align_bytes=64)
+            for h in range(2):
+                acc = psum.tile([P, HALF], F32, name=f"acc_h{t}{h}", tag=f"bank{t}{h}")
+                nc.tensor.matmul_mx(
+                    out=acc[:],
+                    lhsT=d_codes[:, t * P : (t + 1) * P].bitcast(FP8X4),
+                    lhsT_scale=d_planes[:, t * P : (t + 1) * P],
+                    rhs=z_codes[:, cols(h)].bitcast(FP8X4),
+                    rhs_scale=z_planes[:, cols(h)],
+                    start=True,
+                    stop=True,
+                )
+                nc.scalar.activation(neg[:, cols(h)], acc[:], COPY, scale=-0.0625)
+                nc.scalar.activation(pos[:, cols(h)], acc[:], COPY, scale=0.0625)
+            h_neg.append(neg)
+            h_pos.append(pos)
+
+        st = [sb.tile([P, S], F32, name=f"st{t}", align_bytes=64) for t in range(PACK)]
+        other = [sb.tile([P, S], F32, name=f"other{t}", align_bytes=64) for t in range(PACK)]
+        res = [sb.tile([P, S], F32, name=f"res{t}", align_bytes=64) for t in range(PACK)]
+        out_rows = out.rearrange("(p t) n -> t p n", t=PACK)
+
+        def difference(t):
+            for h in range(2):
+                nc.vector.tensor_tensor(
+                    st[t][:, cols(h)], h_neg[t][:].indirect(entries(n3_t, h)), h_pos[t][:, cols(h)], ADD
+                )
+
+        def fetch_other(t, h):
+            nc.vector.tensor_copy(other[t][:, cols(h)], st[t][:].indirect(entries(n4_t, h)))
+
+        def larger(t, span):
+            nc.vector.tensor_tensor(res[t][:, span], other[t][:, span], st[t][:, span], MAX)
+            nc.sync.dma_start(out_rows[t][:, span], res[t][:, span])
+
+        whole = slice(0, S)
+        difference(0)
+        difference(1)
+        fetch_other(0, 0)
+        fetch_other(0, 1)
+        difference(2)
+        larger(0, whole)
+        fetch_other(1, 0)
+        fetch_other(1, 1)
+        difference(3)
+        larger(1, whole)
+        fetch_other(2, 0)
+        fetch_other(2, 1)
+        fetch_other(3, 0)
+        larger(2, whole)
+        fetch_other(3, 1)
+        larger(3, cols(0))
+        larger(3, cols(1))

@@ -52,18 +52,16 @@ def tile_picked_densesumhopmx_none_p_kernel(
 
         w_rows = w1.rearrange("(p j) c -> p j c", j=PACK)
         w_raw = [sb.tile([P, PACK, HALF], F32, name=f"w_raw{h}", align_bytes=64) for h in range(2)]
-        nc.sync.dma_start(w_raw[0][:], w_rows[:, :, cols(0)])
         offs_t = load_list("offs_t", offs)
+        k1_t = load_list("k1_t", k1)
+        nc.sync.dma_start(w_raw[0][:], w_rows[:, :, cols(0)])
         xs_rows = x_scales[0].rearrange("(q i) c -> i q c", i=4)
         for i in range(4):
             nc.sync.dma_start(xs_win[i:P:32, :].bitcast(I32), xs_rows[i].bitcast(I32))
         nc.sync.dma_start(w_raw[1][:], w_rows[:, :, cols(1)])
-        xw_win = sb.tile([P, T], U32, align_bytes=64)
+        nc.sync.dma_start(ds_win[4:P:8, :].bitcast(I32), d_scales[0].bitcast(I32))
+        xw_win = sb.tile([P, T], U32, tag="xw_win", align_bytes=64)
         nc.sync.dma_start(xw_win[:].bitcast(I32), x_words[0].rearrange("p c r -> p (c r)").bitcast(I32))
-        k1_t = load_list("k1_t", k1)
-        ds_rows = d_scales[0].rearrange("(g e) c -> e g c", e=2)
-        for e in range(2):
-            nc.sync.dma_start(ds_win[e:P:16, :].bitcast(I32), ds_rows[e].bitcast(I32))
         gs_t = sb.tile([P, PACK], F32, align_bytes=64)
         nc.sync.dma_start(gs_t[:], gs.rearrange("(p t) o -> p (t o)", t=PACK))
         n2_t = load_list("n2_t", n2)
@@ -82,6 +80,8 @@ def tile_picked_densesumhopmx_none_p_kernel(
             )
         xs_pick = sb.tile([P, S], U8, align_bytes=64)
         nc.vector.tensor_copy(xs_pick[:], xs_win[:].indirect(offs_t[:]))
+        ds_pick = sb.tile([P, H], U8, align_bytes=64)
+        nc.vector.tensor_copy(ds_pick[:], ds_win[:].indirect(k1_t[:]))
         w_codes = sb.tile([P, H], U32, align_bytes=64)
         w_planes = sb.tile([P, H], U8, align_bytes=64)
         nc.vector.quantize_mx(
@@ -91,17 +91,12 @@ def tile_picked_densesumhopmx_none_p_kernel(
         for h in range(2):
             nc.vector.tensor_copy(xw_pick[:, cols(h)], xw_win[:].indirect(entries(offs_t, h)))
 
-        ds_pick = sb.tile([P, H], U8, align_bytes=64)
-        nc.vector.tensor_copy(ds_pick[:], ds_win[:].indirect(k1_t[:]))
-        ds_dealt = sb.tile([P, H], U8, align_bytes=64)
+        ds_dealt = sb.tile([P, H], U8, tag="xw_win", align_bytes=64)
         nc.vector.tensor_copy(
             ds_dealt[:].rearrange("p (t m) -> p m t", t=PACK), ds_pick[:].rearrange("p (m t) -> p m t", t=PACK)
         )
-        for odd in range(2):
-            for e in range(2):
-                nc.sync.dma_start(
-                    d_planes[2 * odd + e : P : 32, :].bitcast(I32), ds_dealt[16 * odd + e : P : 32, :].bitcast(I32)
-                )
+        for i in range(4):
+            nc.sync.dma_start(d_planes[i:P:32, :].bitcast(I32), ds_dealt[8 * i + 4 : P : 32, :].bitcast(I32))
 
         y = []
         for t in range(PACK):
@@ -123,78 +118,98 @@ def tile_picked_densesumhopmx_none_p_kernel(
         z_codes = sb.tile([P, S], U32, align_bytes=64)
         z_planes = sb.tile([P, S], U8, align_bytes=64)
         z = [sb.tile([P, PACK, HALF], F32, name=f"z{h}", align_bytes=64) for h in range(2)]
-        z_bf = [sb.tile([P, HALF, PACK], BF16, name=f"z_bf{h}", align_bytes=64) for h in range(2)]
-        second = {}
+        pieces = [(0, 0, HALF), (1, 0, HALF // 2), (1, HALF // 2, HALF)]
+        z_bf = [
+            sb.tile([P, hi - lo, PACK], BF16, name=f"z_bf{n}", tag=f"z_bf{n}", align_bytes=64)
+            for n, (h, lo, hi) in enumerate(pieces)
+        ]
+        held = {key: sb.tile([P, HALF], F32, name=f"held{key[0]}{key[1]}", tag=f"held{key[0]}{key[1]}", align_bytes=64)
+                for key in [(0, 0), (0, 1), (0, 2), (1, 1), (1, 2)]}
+        second = {key: tile[:] for key, tile in held.items()}
+        second[(0, 3)] = z[1][:, 0, :]
+        second[(1, 3)] = z[1][:, 1, :]
+        second[(1, 0)] = z[1][:, 2, :]
 
         def fetch_second(h, t):
-            tile = sb.tile([P, HALF], F32, name=f"second{h}{t}", tag=f"second{h}{t}", align_bytes=64)
-            nc.vector.tensor_scalar(tile[:], y[t][:].indirect(entries(n2_t, h)), 0.75, 0.0, MULT, ADD)
-            second[(h, t)] = tile
+            nc.vector.tensor_scalar(second[(h, t)], y[t][:].indirect(entries(n2_t, h)), 0.75, 0.0, MULT, ADD)
 
         def fetch_first(h, t):
-            nc.vector.tensor_tensor(z[h][:, t, :], y[t][:].indirect(entries(n1_t, h)), second[(h, t)][:], ADD)
-            if t == PACK - 1:
-                nc.scalar.copy(
-                    z_bf[h][:].rearrange("p (c i) t -> p c t i", i=4),
-                    z[h][:].rearrange("p t (c i) -> p c t i", i=4),
-                )
+            nc.vector.tensor_tensor(z[h][:, t, :], y[t][:].indirect(entries(n1_t, h)), second[(h, t)], ADD)
 
-        def quantise_z(h):
-            nc.vector.quantize_mx(
-                out=z_codes[:, cols(h)].bitcast(FP8X4),
-                scales=z_planes[:, cols(h)],
-                in_=z_bf[h][:].rearrange("p n t -> p (n t)"),
+        def weave_z(n):
+            h, lo, hi = pieces[n]
+            nc.scalar.copy(
+                z_bf[n][:].rearrange("p (c i) t -> p c t i", i=4),
+                z[h][:, :, lo:hi].rearrange("p t (c i) -> p c t i", i=4),
             )
 
-        steps = [(h, t) for h in range(2) for t in range(PACK)]
-        fetch_second(*steps[0])
-        for s in range(1, len(steps)):
-            fetch_second(*steps[s])
-            fetch_first(*steps[s - 1])
-        fetch_first(*steps[-1])
-        quantise_z(0)
+        def quantise_z(n):
+            h, lo, hi = pieces[n]
+            span = slice(h * HALF + lo, h * HALF + hi)
+            nc.vector.quantize_mx(
+                out=z_codes[:, span].bitcast(FP8X4),
+                scales=z_planes[:, span],
+                in_=z_bf[n][:].rearrange("p n t -> p (n t)"),
+            )
 
-        dw_pick = sb.tile([P, H], U32, tag="second12", align_bytes=64)
-        nc.vector.tensor_copy(dw_pick[:], dw_win[:].indirect(k1_t[:]))
-        d_codes = sb.tile([P, H], U32, align_bytes=64)
-        nc.vector.tensor_copy(
-            d_codes[:].rearrange("p (t m) -> p m t", t=PACK), dw_pick[:].rearrange("p (m t) -> p m t", t=PACK)
-        )
-        quantise_z(1)
-
-        h_neg, h_pos = [], []
         for t in range(PACK):
-            neg = sb.tile([P, S], F32, name=f"h_neg{t}", align_bytes=64)
-            pos = sb.tile([P, S], F32, name=f"h_pos{t}", align_bytes=64)
-            for h in range(2):
-                acc = psum.tile([P, HALF], F32, name=f"acc_h{t}{h}", tag=f"bank{t}{h}")
-                nc.tensor.matmul_mx(
-                    out=acc[:],
-                    lhsT=d_codes[:, t * P : (t + 1) * P].bitcast(FP8X4),
-                    lhsT_scale=d_planes[:, t * P : (t + 1) * P],
-                    rhs=z_codes[:, cols(h)].bitcast(FP8X4),
-                    rhs_scale=z_planes[:, cols(h)],
-                    start=True,
-                    stop=True,
-                )
-                nc.scalar.activation(neg[:, cols(h)], acc[:], COPY, scale=-0.0625)
-                nc.scalar.activation(pos[:, cols(h)], acc[:], COPY, scale=0.0625)
-            h_neg.append(neg)
-            h_pos.append(pos)
+            fetch_second(0, t)
+            fetch_second(1, t)
+            fetch_first(0, t)
+        weave_z(0)
+        for t in (3, 0, 1, 2):
+            fetch_first(1, t)
+        weave_z(1)
+        weave_z(2)
 
-        st = [sb.tile([P, S], F32, name=f"st{t}", align_bytes=64) for t in range(PACK)]
+        dw_pick = sb.tile([P, H], U32, tag="held11", align_bytes=64)
+        nc.vector.tensor_copy(dw_pick[:], dw_win[:].indirect(k1_t[:]))
+        d_codes = []
+
+        def deal_words(u, tag):
+            tile = sb.tile([P, 2 * P], U32, name=f"d_codes{u}", tag=tag, align_bytes=64)
+            nc.vector.tensor_copy(
+                tile[:].rearrange("p (t m) -> p m t", t=2),
+                dw_pick[:].rearrange("p (m t) -> p m t", t=PACK)[:, :, 2 * u : 2 * u + 2],
+            )
+            d_codes.append(tile)
+
+        quantise_z(0)
+        deal_words(0, "d_codes0")
+        quantise_z(1)
+        quantise_z(2)
+        deal_words(1, "z_bf2")
+
+        h_neg = [sb.tile([P, 2 * S], F32, name=f"h_neg{t}", align_bytes=64) for t in range(PACK)]
+        h_pos = [sb.tile([P, S], F32, name=f"h_pos{t}", align_bytes=64) for t in range(PACK)]
+        groups = [(0, 0, 256), (1, 0, 256), (0, 256, 384), (0, 384, 512), (1, 256, 512), (2, 0, 512), (3, 0, 512)]
+        for n, (t, lo, hi) in enumerate(groups):
+            acc = psum.tile([P, hi - lo], F32, name=f"acc_h{n}", tag=f"bank{n // 2}{n % 2}")
+            nc.tensor.matmul_mx(
+                out=acc[:],
+                lhsT=d_codes[t // 2][:, (t % 2) * P : (t % 2 + 1) * P].bitcast(FP8X4),
+                lhsT_scale=d_planes[:, t * P : (t + 1) * P],
+                rhs=z_codes[:, lo:hi].bitcast(FP8X4),
+                rhs_scale=z_planes[:, lo:hi],
+                start=True,
+                stop=True,
+            )
+            nc.scalar.activation(h_neg[t][:, lo:hi], acc[:], COPY, scale=-0.0625)
+            nc.scalar.activation(h_pos[t][:, lo:hi], acc[:], COPY, scale=0.0625)
+
+        st = [sb.tile([P, 2 * S], F32, name=f"st{t}", align_bytes=64) for t in range(PACK)]
         other = [sb.tile([P, S], F32, name=f"other{t}", align_bytes=64) for t in range(PACK)]
         res = [sb.tile([P, S], F32, name=f"res{t}", align_bytes=64) for t in range(PACK)]
         out_rows = out.rearrange("(p t) n -> t p n", t=PACK)
 
         def difference(t):
-            for h in range(2):
-                nc.vector.tensor_tensor(
-                    st[t][:, cols(h)], h_neg[t][:].indirect(entries(n3_t, h)), h_pos[t][:, cols(h)], ADD
-                )
+            nc.vector.tensor_tensor(st[t][:, 0:S], h_neg[t][:].indirect(n3_t[:]), h_pos[t][:], ADD)
 
         def fetch_other(t, h):
             nc.vector.tensor_copy(other[t][:, cols(h)], st[t][:].indirect(entries(n4_t, h)))
+
+        def fetch_all_other(t):
+            nc.vector.tensor_copy(other[t][:], st[t][:].indirect(n4_t[:]))
 
         def larger(t, span):
             nc.vector.tensor_tensor(res[t][:, span], other[t][:, span], st[t][:, span], MAX)
@@ -203,16 +218,13 @@ def tile_picked_densesumhopmx_none_p_kernel(
         whole = slice(0, S)
         difference(0)
         difference(1)
-        fetch_other(0, 0)
-        fetch_other(0, 1)
+        fetch_all_other(0)
         difference(2)
         larger(0, whole)
-        fetch_other(1, 0)
-        fetch_other(1, 1)
+        fetch_all_other(1)
         difference(3)
         larger(1, whole)
-        fetch_other(2, 0)
-        fetch_other(2, 1)
+        fetch_all_other(2)
         fetch_other(3, 0)
         larger(2, whole)
         fetch_other(3, 1)

from contextlib import ExitStack

import concourse.mybir as mybir

K, T, S, H, G = 512, 2048, 512, 512, 2048
FLOPS = 2 * K * H * S + 2 * K * H * S

F32 = mybir.dt.float32
BF16 = mybir.dt.bfloat16
I32 = mybir.dt.int32
U32 = mybir.dt.uint32
U16 = mybir.dt.uint16
U8 = mybir.dt.uint8
FP8X4 = mybir.dt.float8_e4m3fn_x4
COPY = mybir.ActivationFunctionType.Copy
MULT = mybir.AluOpType.mult
ADD = mybir.AluOpType.add
MAX = mybir.AluOpType.max

P = 128
PACK = 4
HALF = S // 2
LCOL = HALF // 16


def tile_picked_densesumhopmx_none_p_kernel(
    tc, x_words, x_scales, w1, gs, d_words, d_scales, offs, n1, n2, k1, n3, n4, out
):
    nc = tc.nc
    with ExitStack() as ctx:
        lists = ctx.enter_context(tc.tile_pool(name="lists", bufs=1))
        sb = ctx.enter_context(tc.tile_pool(name="sb", bufs=1))
        psum = ctx.enter_context(tc.psum_pool(name="psum", bufs=1))

        def cols(h):
            return slice(h * HALF, (h + 1) * HALF)

        def entries(tile, h):
            return tile[:, h * LCOL : (h + 1) * LCOL]

        def load_list(name, src):
            tile = lists.tile([P, S // 16], U16, name=name)
            nc.sync.dma_start(tile[:], src)
            return tile

        xs_win = sb.tile([P, T], U8, align_bytes=64)
        nc.gpsimd.memset(xs_win[:].bitcast(I32), 0)
        ds_win = sb.tile([P, G], U8, align_bytes=64)
        nc.vector.memset(ds_win[:].bitcast(I32), 0)
        d_planes = sb.tile([P, H], U8, align_bytes=64)
        nc.gpsimd.memset(d_planes[:].bitcast(I32), 0)

        w_rows = w1.rearrange("(p j) c -> p j c", j=PACK)
        w_raw = [sb.tile([P, PACK, HALF], F32, name=f"w_raw{h}", align_bytes=64) for h in range(2)]
        offs_t = load_list("offs_t", offs)
        k1_t = load_list("k1_t", k1)
        nc.sync.dma_start(w_raw[0][:], w_rows[:, :, cols(0)])
        xs_rows = x_scales[0].rearrange("(q i) c -> i q c", i=4)
        for i in range(4):
            nc.sync.dma_start(xs_win[i:P:32, :].bitcast(I32), xs_rows[i].bitcast(I32))
        nc.sync.dma_start(w_raw[1][:], w_rows[:, :, cols(1)])
        nc.sync.dma_start(ds_win[4:P:8, :].bitcast(I32), d_scales[0].bitcast(I32))
        xw_win = sb.tile([P, T], U32, tag="xw_win", align_bytes=64)
        nc.sync.dma_start(xw_win[:].bitcast(I32), x_words[0].rearrange("p c r -> p (c r)").bitcast(I32))
        gs_t = sb.tile([P, PACK], F32, align_bytes=64)
        nc.sync.dma_start(gs_t[:], gs.rearrange("(p t) o -> p (t o)", t=PACK))
        n2_t = load_list("n2_t", n2)
        n1_t = load_list("n1_t", n1)
        dw_win = sb.tile([P, G], U32, align_bytes=64)
        nc.sync.dma_start(dw_win[:].bitcast(I32), d_words[0].rearrange("p c r -> p (c r)").bitcast(I32))
        n3_t = load_list("n3_t", n3)
        n4_t = load_list("n4_t", n4)

        w_bf = sb.tile([P, PACK, P, PACK], BF16, align_bytes=64)
        for h in range(2):
            nc.scalar.activation(
                w_bf[:, :, h * (P // 2) : (h + 1) * (P // 2), :].rearrange("p t m j -> p m j t"),
                w_raw[h][:].rearrange("p j (m t) -> p m j t", t=PACK),
                COPY,
            )
        xs_pick = sb.tile([P, S], U8, align_bytes=64)
        nc.vector.tensor_copy(xs_pick[:], xs_win[:].indirect(offs_t[:]))
        ds_pick = sb.tile([P, H], U8, align_bytes=64)
        nc.vector.tensor_copy(ds_pick[:], ds_win[:].indirect(k1_t[:]))
        w_codes = sb.tile([P, H], U32, align_bytes=64)
        w_planes = sb.tile([P, H], U8, align_bytes=64)
        nc.vector.quantize_mx(
            out=w_codes[:].bitcast(FP8X4), scales=w_planes[:], in_=w_bf[:].rearrange("p t m j -> p (t m j)")
        )
        xw_pick = sb.tile([P, S], U32, align_bytes=64)
        for h in range(2):
            nc.vector.tensor_copy(xw_pick[:, cols(h)], xw_win[:].indirect(entries(offs_t, h)))

        ds_dealt = sb.tile([P, H], U8, tag="xw_win", align_bytes=64)
        nc.vector.tensor_copy(
            ds_dealt[:].rearrange("p (t m) -> p m t", t=PACK), ds_pick[:].rearrange("p (m t) -> p m t", t=PACK)
        )
        for i in range(4):
            nc.sync.dma_start(d_planes[i:P:32, :].bitcast(I32), ds_dealt[8 * i + 4 : P : 32, :].bitcast(I32))

        y = []
        for t in range(PACK):
            y_t = sb.tile([P, S], F32, name=f"y{t}", align_bytes=64)
            for h in range(2):
                acc = psum.tile([P, HALF], F32, name=f"acc_y{t}{h}", tag=f"bank{t}{h}")
                nc.tensor.matmul_mx(
                    out=acc[:],
                    lhsT=w_codes[:, t * P : (t + 1) * P].bitcast(FP8X4),
                    lhsT_scale=w_planes[:, t * P : (t + 1) * P],
                    rhs=xw_pick[:, cols(h)].bitcast(FP8X4),
                    rhs_scale=xs_pick[:, cols(h)],
                    start=True,
                    stop=True,
                )
                nc.scalar.activation(y_t[:, cols(h)], acc[:], COPY, scale=gs_t[:, t : t + 1])
            y.append(y_t)

        z_codes = sb.tile([P, S], U32, align_bytes=64)
        z_planes = sb.tile([P, S], U8, align_bytes=64)
        z = [sb.tile([P, PACK, HALF], F32, name=f"z{h}", align_bytes=64) for h in range(2)]
        pieces = [(0, 0, HALF), (1, 0, HALF // 2), (1, HALF // 2, HALF)]
        z_bf = [
            sb.tile([P, hi - lo, PACK], BF16, name=f"z_bf{n}", tag=f"z_bf{n}", align_bytes=64)
            for n, (h, lo, hi) in enumerate(pieces)
        ]
        held = {key: sb.tile([P, HALF], F32, name=f"held{key[0]}{key[1]}", tag=f"held{key[0]}{key[1]}", align_bytes=64)
                for key in [(0, 0), (0, 1), (0, 2), (1, 1), (1, 2)]}
        second = {key: tile[:] for key, tile in held.items()}
        second[(0, 3)] = z[1][:, 0, :]
        second[(1, 3)] = z[1][:, 1, :]
        second[(1, 0)] = z[1][:, 2, :]

        def fetch_second(h, t):
            nc.vector.tensor_scalar(second[(h, t)], y[t][:].indirect(entries(n2_t, h)), 0.75, 0.0, MULT, ADD)

        def fetch_first(h, t):
            nc.vector.tensor_tensor(z[h][:, t, :], y[t][:].indirect(entries(n1_t, h)), second[(h, t)], ADD)

        def weave_z(n):
            h, lo, hi = pieces[n]
            nc.scalar.copy(
                z_bf[n][:].rearrange("p (c i) t -> p c t i", i=4),
                z[h][:, :, lo:hi].rearrange("p t (c i) -> p c t i", i=4),
            )

        def quantise_z(n):
            h, lo, hi = pieces[n]
            span = slice(h * HALF + lo, h * HALF + hi)
            nc.vector.quantize_mx(
                out=z_codes[:, span].bitcast(FP8X4),
                scales=z_planes[:, span],
                in_=z_bf[n][:].rearrange("p n t -> p (n t)"),
            )

        for t in range(PACK):
            fetch_second(0, t)
            fetch_second(1, t)
            fetch_first(0, t)
        weave_z(0)
        for t in (3, 0, 1, 2):
            fetch_first(1, t)
        weave_z(1)
        weave_z(2)

        dw_pick = sb.tile([P, H], U32, tag="held11", align_bytes=64)
        nc.vector.tensor_copy(dw_pick[:], dw_win[:].indirect(k1_t[:]))
        d_codes = []

        def deal_words(u, tag):
            tile = sb.tile([P, 2 * P], U32, name=f"d_codes{u}", tag=tag, align_bytes=64)
            nc.vector.tensor_copy(
                tile[:].rearrange("p (t m) -> p m t", t=2),
                dw_pick[:].rearrange("p (m t) -> p m t", t=PACK)[:, :, 2 * u : 2 * u + 2],
            )
            d_codes.append(tile)

        quantise_z(0)
        deal_words(0, "d_codes0")
        quantise_z(1)
        quantise_z(2)
        deal_words(1, "z_bf2")

        h_neg = [sb.tile([P, 2 * S], F32, name=f"h_neg{t}", align_bytes=64) for t in range(PACK)]
        h_pos = [sb.tile([P, S], F32, name=f"h_pos{t}", align_bytes=64) for t in range(PACK)]
        groups = [(0, 0, 256), (1, 0, 256), (0, 256, 384), (0, 384, 512), (1, 256, 512), (2, 0, 512), (3, 0, 512)]
        for n, (t, lo, hi) in enumerate(groups):
            acc = psum.tile([P, hi - lo], F32, name=f"acc_h{n}", tag=f"bank{n // 2}{n % 2}")
            nc.tensor.matmul_mx(
                out=acc[:],
                lhsT=d_codes[t // 2][:, (t % 2) * P : (t % 2 + 1) * P].bitcast(FP8X4),
                lhsT_scale=d_planes[:, t * P : (t + 1) * P],
                rhs=z_codes[:, lo:hi].bitcast(FP8X4),
                rhs_scale=z_planes[:, lo:hi],
                start=True,
                stop=True,
            )
            nc.scalar.activation(h_neg[t][:, lo:hi], acc[:], COPY, scale=-0.0625)
            nc.scalar.activation(h_pos[t][:, lo:hi], acc[:], COPY, scale=0.0625)

        st = [sb.tile([P, 2 * S], F32, name=f"st{t}", align_bytes=64) for t in range(PACK)]
        other = [sb.tile([P, S], F32, name=f"other{t}", align_bytes=64) for t in range(PACK)]
        res = [sb.tile([P, S], F32, name=f"res{t}", align_bytes=64) for t in range(PACK)]
        out_rows = out.rearrange("(p t) n -> t p n", t=PACK)

        def difference(t):
            nc.vector.tensor_tensor(st[t][:, 0:S], h_neg[t][:].indirect(n3_t[:]), h_pos[t][:], ADD)

        def fetch_other(t, h):
            nc.vector.tensor_copy(other[t][:, cols(h)], st[t][:].indirect(entries(n4_t, h)))

        def fetch_all_other(t):
            nc.vector.tensor_copy(other[t][:], st[t][:].indirect(n4_t[:]))

        def larger(t, span):
            nc.vector.tensor_tensor(res[t][:, span], other[t][:, span], st[t][:, span], MAX)
            nc.sync.dma_start(out_rows[t][:, span], res[t][:, span])

        whole = slice(0, S)
        difference(0)
        difference(1)
        fetch_all_other(0)
        difference(2)
        larger(0, whole)
        fetch_all_other(1)
        difference(3)
        larger(1, whole)
        fetch_all_other(2)
        fetch_other(3, 0)
        larger(2, whole)
        fetch_other(3, 1)
        larger(3, cols(0))
        larger(3, cols(1))
